import numpy as np
import ml_dtypes


def mxq(x, axis, fmt="e4m3"):
    dtype, down = {"e4m3": (ml_dtypes.float8_e4m3fn, 7), "e5m2": (ml_dtypes.float8_e5m2, 14)}[fmt]
    v = np.moveaxis(np.asarray(x, np.float32).astype(ml_dtypes.bfloat16).astype(np.float64), axis, -1)
    blocks = v.reshape(v.shape[:-1] + (-1, 32))
    amax = np.abs(blocks).max(-1, keepdims=True)
    byte = np.maximum(np.where(amax > 0, np.frexp(amax)[1] - 1 + 127, 0) - down, 1)
    scale = np.exp2(byte - 127.0)
    codes = (blocks / scale).astype(np.float32).astype(dtype).astype(np.float64)
    return np.moveaxis((codes * scale).reshape(v.shape), -1, axis)


WIDE = False


def mx_kscale(k):
    if not WIDE:
        return np.ones(k)
    levels = np.array([10, -10, 5, -5, 0])
    if k % 512:
        return np.exp2(np.random.permutation(np.resize(levels, k // 32))).repeat(32)
    a = np.empty((k // 512, 16))
    for p in range(k // 512):
        a[p, :8] = np.random.permutation(np.resize(levels, 8))
        for g in range(8):
            far = levels[np.abs(levels - a[p, g]) >= 10]
            a[p, g + 8] = far[np.random.randint(len(far))]
    return np.exp2(a.ravel()).repeat(32)


def f64(x):
    return np.asarray(x).astype(np.float64)


def striped(idx):
    return np.tile(idx.reshape(-1, 16).T, (8, 1)).astype(np.uint16)


def unstriped(offs):
    return offs[:16].T.reshape(-1).astype(np.int64)


def striped8(idx):
    return np.concatenate([x.reshape(-1, 16).T for x in idx]).astype(np.uint16)


def runs(offs, k):
    lists = np.stack([offs[16 * r : 16 * r + 16].T.reshape(-1) for r in range(8)]).astype(np.int64)
    return lists[np.arange(k) % 512 // 64]


def pack_weight(w):
    k, n = w.shape
    w = f64(np.asarray(w, np.float32).astype(ml_dtypes.bfloat16)).reshape(k // 32, 32, n)
    amax = np.abs(w).max(1)
    byte = np.clip(np.where(amax > 0, np.frexp(amax)[1] - 1 + 127 - 7, 1), 1, 254)
    scaled = (w * np.exp2(127.0 - byte)[:, None, :]).reshape(k, n).astype(np.float32)
    words = np.ascontiguousarray(scaled.reshape(k // 512, 128, 4, n).transpose(0, 1, 3, 2)).astype(ml_dtypes.float8_e4m3fn).view(np.uint8)
    return words, np.ascontiguousarray(byte.astype(np.uint8).reshape(k // 512, 16, n))


def unpack_weight(words, scales):
    g, p, n, _ = words.shape
    vals = np.ascontiguousarray(words).view(ml_dtypes.float8_e4m3fn).astype(np.float64) * np.repeat(np.exp2(scales.astype(np.float64) - 127.0), 8, axis=1)[..., None]
    return vals.transpose(0, 1, 3, 2).reshape(g * 512, n)


E2M1 = np.array([0.0, 0.5, 1.0, 1.5, 2.0, 3.0, 4.0, 6.0, -0.0, -0.5, -1.0, -1.5, -2.0, -3.0, -4.0, -6.0])


def pack_fp4(w):
    k, n = w.shape
    w = f64(np.asarray(w, np.float32).astype(ml_dtypes.bfloat16)).reshape(k // 32, 32, n)
    amax = np.abs(w).max(1)
    mant, ex = np.frexp(amax / 6.0)
    byte = np.clip(np.where(amax > 0, np.where(mant > 0.5, ex, ex - 1) + 127, 1), 1, 254)
    scaled = (w * np.exp2(127.0 - byte)[:, None, :]).reshape(k, n).astype(np.float32)
    c = np.ascontiguousarray(scaled.reshape(k // 512, 128, 4, n).transpose(0, 1, 3, 2)).astype(ml_dtypes.float4_e2m1fn).view(np.uint8) & 0xF
    words = (c[..., 0::2] | (c[..., 1::2] << 4)).reshape(k // 512, 128, 2 * n)
    return np.ascontiguousarray(words), np.ascontiguousarray(byte.astype(np.uint8).reshape(k // 512, 16, n))


def unpack_fp4(words, scales):
    g, _, n = scales.shape
    words = np.ascontiguousarray(words).reshape(g, 128, n, 2)
    nib = np.empty((g, 128, n, 4), np.uint8)
    nib[..., 0::2] = words & 0xF
    nib[..., 1::2] = words >> 4
    vals = E2M1[nib] * np.repeat(np.exp2(scales.astype(np.float64) - 127.0), 8, axis=1)[..., None]
    return vals.transpose(0, 1, 3, 2).reshape(g * 512, n)


K, T, S, H, G, W = 512, 1024, 256, 512, 2048, 128


def setup_inputs():
    n = np.random.standard_normal
    s = mx_kscale(K)[:, None]
    packed_xT = pack_weight(n((K, T)) * s)
    packed_w1 = pack_fp4(n((K, H)) / np.sqrt(K) / s)
    packed_dT = pack_weight(n((K, G)) / s)
    perm = np.random.permutation(S)
    return {
        "x_words": packed_xT[0],
        "x_scales": packed_xT[1],
        "w1_words": packed_w1[0],
        "w1_scales": packed_w1[1],
        "gs": (np.random.uniform(0.5, 1.5, (K, 1)) * s).astype(np.float32),
        "d_words": packed_dT[0],
        "d_scales": packed_dT[1],
        "offs": striped(np.random.permutation(T)[:S]),
        "k1": striped8(np.random.randint(0, G, (8, H))),
        "k2": striped8(np.random.randint(0, G, (8, H))),
        "hz": striped8(np.random.randint(0, T, (8, S))),
        "n1": striped(perm[:W]),
        "n2": striped(perm[W:]),
        "n3": striped(np.random.permutation(S)),
    }


def reference(x_words, x_scales, w1_words, w1_scales, gs, d_words, d_scales, offs, k1, k2, hz, n1, n2, n3):
    d_k1 = unpack_weight(d_words, d_scales)[np.arange(K)[:, None], runs(k1, K)]
    xq = unpack_weight(x_words, x_scales)[:, unstriped(offs)]
    y = unpack_fp4(w1_words, w1_scales).T @ xq
    z = f64(gs) * y
    d_k2 = unpack_weight(d_words, d_scales)[np.arange(K)[:, None], runs(k2, K)]
    x_hz = unpack_weight(x_words, x_scales)[np.arange(K)[:, None], runs(hz, K)]
    h = 0.0625 * ((d_k1.T @ mxq(z, 0, "e4m3") + d_k2.T @ x_hz))
    pa = h[:, unstriped(n1)]
    pb = h[:, unstriped(n2)]
    rb = pa - pb
    ds = np.zeros((H, S))
    ds[:, unstriped(n1)] = pb
    dt = ds.copy()
    dt[:, unstriped(n2)] = rb
    return np.maximum(dt, 0.5 * dt[:, unstriped(n3)])

@@ -1,0 +1,186 @@
+from contextlib import ExitStack
+
+import concourse.mybir as mybir
+
+K, T, S, H, G, W = 512, 1024, 256, 512, 2048, 128
+FLOPS = 3 * 2 * K * H * S
+
+F32 = mybir.dt.float32
+BF16 = mybir.dt.bfloat16
+I32 = mybir.dt.int32
+U32 = mybir.dt.uint32
+U16 = mybir.dt.uint16
+U8 = mybir.dt.uint8
+FP8X4 = mybir.dt.float8_e4m3fn_x4
+FP4X4 = mybir.dt.float4_e2m1fn_x4
+COPY = mybir.ActivationFunctionType.Copy
+ALU = mybir.AluOpType
+
+P = 128
+HALF = 256
+SPARE = 8
+
+
+def tile_picked_cmixhiswapd_none_p_kernel(
+    tc, x_words, x_scales, w1_words, w1_scales, gs, d_words, d_scales, offs, k1, k2, hz, n1, n2, n3, out
+):
+    nc = tc.nc
+    with ExitStack() as ctx:
+        keep = ctx.enter_context(tc.tile_pool(name="keep", bufs=1))
+        psum = ctx.enter_context(tc.psum_pool(name="psum", bufs=1))
+
+        def sb(name, shape, dtype):
+            return keep.tile(shape, dtype, name=name, align_bytes=64)
+
+        def load_list(name, src):
+            t = keep.tile(list(src.shape), U16, name=name)
+            nc.sync.dma_start(t[:], src)
+            return t
+
+        def load_scale_window(name, src, cols):
+            t = sb(name, [P, cols], U8)
+            rows = src[0].bitcast(I32).unsqueeze(1).broadcast_to([16, 8, cols // 4])
+            nc.scalar.dma_start(t[:].bitcast(I32), rows)
+            return t
+
+        def load_words(name, src, cols):
+            t = sb(name, [P, cols], U32)
+            nc.sync.dma_start(t[:].bitcast(I32), src[0].rearrange("p n t -> p (n t)").bitcast(I32))
+            return t
+
+        w1s_raw = sb("w1s_raw", [P, H], U8)
+        nc.vector.memset(w1s_raw[:].bitcast(I32), 0)
+
+        w1w_raw = sb("w1w_raw", [P, 2 * H], U8)
+        nc.gpsimd.dma_start(w1w_raw[:].bitcast(I32), w1_words[0].bitcast(I32))
+        offs_t = load_list("offs_t", offs)
+        xs_win = load_scale_window("xs_win", x_scales, T)
+        hz_t = load_list("hz_t", hz)
+        ds_win = load_scale_window("ds_win", d_scales, G)
+        k1_t = load_list("k1_t", k1)
+        k2_t = load_list("k2_t", k2)
+        xw_win = load_words("xw_win", x_words, T)
+        dw_win = load_words("dw_win", d_words, G)
+        for j in range(4):
+            nc.scalar.dma_start(w1s_raw[j:P:32, :].bitcast(I32), w1_scales[0, j:16:4, :].bitcast(I32))
+        n1_t = load_list("n1_t", n1)
+        n2_t = load_list("n2_t", n2)
+        gs_t = sb("gs_t", [P, 4], F32)
+        nc.sync.dma_start(gs_t[:], gs.rearrange("(p t) o -> p (t o)", t=4))
+        n3_t = load_list("n3_t", n3)
+
+        def gather(dst, window, lst):
+            nc.vector.tensor_copy(dst, window[:].indirect(lst))
+
+        def place_scales(name, picked, cols, queue):
+            plane = sb(name, [P, cols], U8)
+            nc.vector.tensor_copy(plane[:].bitcast(I32), picked[:].bitcast(I32))
+            for j in range(1, 4):
+                queue.dma_start(plane[j:P:32, :].bitcast(I32), picked[8 * j : P : 32, :].bitcast(I32))
+            return plane
+
+        xq_pick = sb("xq_pick", [P, S], U8)
+        gather(xq_pick[:], xs_win, offs_t[:])
+        xq_s = place_scales("xq_s", xq_pick, S, nc.scalar)
+
+        first_pick = sb("first_pick", [P, S + 2 * HALF], U8)
+        gather(first_pick[:, 0:S], xs_win, hz_t[:])
+        xq_w = sb("xq_w", [P, S], U32)
+        gather(xq_w[:], xw_win, offs_t[:])
+
+        w1w = sb("w1w", [P, 2 * H], U8)
+        nc.scalar.copy(
+            w1w[:].bitcast(U16).rearrange("p (t m) -> p t m", t=4),
+            w1w_raw[:].bitcast(U16).rearrange("p (m t) -> p t m", t=4),
+        )
+        w1s = sb("w1s", [P, H], U8)
+        nc.vector.tensor_copy(w1s[:].rearrange("p (t m) -> p t m", t=4), w1s_raw[:].rearrange("p (m t) -> p t m", t=4))
+
+        lc = HALF // 16
+        gather(first_pick[:, S : S + HALF], ds_win, k1_t[:, 0:lc])
+        gather(first_pick[:, S + HALF :], ds_win, k2_t[:, 0:lc])
+        first_s = place_scales("first_s", first_pick, S + 2 * HALF, nc.scalar)
+
+        z_rows = sb("z_rows", [P, 4, S], BF16)
+        for t in range(4):
+            y = psum.tile([P, S], F32, name=f"y{t}")
+            nc.tensor.matmul_mx(
+                out=y[:],
+                lhsT=w1w[:, 2 * P * t : 2 * P * (t + 1)].bitcast(FP4X4),
+                lhsT_scale=w1s[:, P * t : P * (t + 1)],
+                rhs=xq_w[:].bitcast(FP8X4),
+                rhs_scale=xq_s[:],
+                start=True,
+                stop=True,
+            )
+            nc.scalar.activation(z_rows[:, t, :], y[:], COPY, scale=gs_t[:, t : t + 1])
+        z_packed = sb("z_packed", [P, S, 4], BF16)
+        nc.scalar.copy(z_packed[:], z_rows[:].rearrange("p t n -> p n t"))
+
+        xh_w = sb("xh_w", [P, S], U32)
+        gather(xh_w[:], xw_win, hz_t[:])
+        d1_w = [sb(f"d1_w{u}", [P, HALF], U32) for u in range(2)]
+        d2_w = [sb(f"d2_w{u}", [P, HALF], U32) for u in range(2)]
+        gather(d2_w[0][:], dw_win, k2_t[:, 0:lc])
+        gather(d1_w[0][:], dw_win, k1_t[:, 0:lc])
+
+        z_w = sb("z_w", [P, S], U32)
+        z_s = sb("z_s", [P, S], U8)
+        nc.vector.quantize_mx(out=z_w[:].bitcast(FP8X4), scales=z_s[:], in_=z_packed[:].rearrange("p n t -> p (n t)"))
+
+        def second_product(i, d1_s, d2_s):
+            u, c = divmod(i, 2)
+            cols = slice(P * c, P * (c + 1))
+            acc = psum.tile([P, S], F32, name=f"h{i}")
+            nc.tensor.matmul_mx(
+                out=acc[:], lhsT=d2_w[u][:, cols].bitcast(FP8X4), lhsT_scale=d2_s[:, cols],
+                rhs=xh_w[:].bitcast(FP8X4), rhs_scale=first_s[:, 0:S], start=True, stop=False,
+            )
+            nc.tensor.matmul_mx(
+                out=acc[:], lhsT=d1_w[u][:, cols].bitcast(FP8X4), lhsT_scale=d1_s[:, cols],
+                rhs=z_w[:].bitcast(FP8X4), rhs_scale=z_s[:], start=False, stop=True,
+            )
+            h = sb(f"h_sb{i}", [P, S], F32)
+            nc.vector.tensor_scalar_mul(h[:], acc[:], 0.0625)
+            return h
+
+        def fetch_pairs(i, h):
+            pb = sb(f"pb{i}", [P, W], F32)
+            pa = sb(f"pa{i}", [P, W], F32)
+            rb = sb(f"rb{i}", [P, W], F32)
+            nc.scalar.activation(pb[:], h[:].indirect(n2_t[:]), COPY)
+            nc.scalar.activation(pa[:], h[:].indirect(n1_t[:]), COPY)
+            nc.vector.tensor_tensor(rb[:], pa[:], pb[:], ALU.subtract)
+            return pb, rb
+
+        def put_back(i, pb, rb):
+            dt = sb(f"dt{i}", [P, S + SPARE], F32)
+            nc.gpsimd.memset(dt[:, S:], 0.0)
+            nc.scalar.activation(dt[:].indirect(n1_t[:]), pb[:], COPY)
+            nc.scalar.activation(dt[:].indirect(n2_t[:]), rb[:], COPY)
+            return dt
+
+        def finish(i, dt):
+            far = sb(f"far{i}", [P, S], F32)
+            nc.scalar.activation(far[:], dt[:].indirect(n3_t[:]), COPY)
+            res = sb(f"res{i}", [P, S], F32)
+            nc.vector.scalar_tensor_tensor(res[:], far[:], 0.5, dt[:, 0:S], ALU.mult, ALU.max)
+            nc.sync.dma_start(out[P * i : P * (i + 1), :], res[:])
+
+        hs = [second_product(i, first_s[:, S : S + HALF], first_s[:, S + HALF :]) for i in range(2)]
+        pairs = [fetch_pairs(i, hs[i]) for i in range(2)]
+
+        second_pick = sb("second_pick", [P, 2 * HALF], U8)
+        gather(second_pick[:, 0:HALF], ds_win, k1_t[:, lc:])
+        gather(second_pick[:, HALF:], ds_win, k2_t[:, lc:])
+        second_s = place_scales("second_s", second_pick, 2 * HALF, nc.sync)
+        gather(d2_w[1][:], dw_win, k2_t[:, lc:])
+        gather(d1_w[1][:], dw_win, k1_t[:, lc:])
+
+        dts = [put_back(i, *pairs[i]) for i in range(2)]
+        for i in range(2):
+            finish(i, dts[i])
+        hs = [second_product(i, second_s[:, 0:HALF], second_s[:, HALF:]) for i in range(2, 4)]
+        pairs = [fetch_pairs(i, hs[i - 2]) for i in range(2, 4)]
+        for i in range(2, 4):
+            finish(i, put_back(i, *pairs[i - 2]))

@@ -29,44 +29,51 @@ def tile_picked_cmixhiswapd_none_p_kernel(
         keep = ctx.enter_context(tc.tile_pool(name="keep", bufs=1))
         psum = ctx.enter_context(tc.psum_pool(name="psum", bufs=1))
 
-        def sb(name, shape, dtype):
-            return keep.tile(shape, dtype, name=name, align_bytes=64)
+        def sb(name, shape, dtype, tag=None):
+            return keep.tile(shape, dtype, name=name, tag=tag or name, align_bytes=64)
 
         def load_list(name, src):
             t = keep.tile(list(src.shape), U16, name=name)
             nc.sync.dma_start(t[:], src)
             return t
 
-        def load_scale_window(name, src, cols):
+        def load_scale_window(name, src, cols, queue):
             t = sb(name, [P, cols], U8)
             rows = src[0].bitcast(I32).unsqueeze(1).broadcast_to([16, 8, cols // 4])
-            nc.scalar.dma_start(t[:].bitcast(I32), rows)
+            queue.dma_start(t[:].bitcast(I32), rows)
             return t
 
-        def load_words(name, src, cols):
-            t = sb(name, [P, cols], U32)
+        def load_words(name, src, cols, tag=None):
+            t = sb(name, [P, cols], U32, tag=tag)
             nc.sync.dma_start(t[:].bitcast(I32), src[0].rearrange("p n t -> p (n t)").bitcast(I32))
             return t
 
-        w1s_raw = sb("w1s_raw", [P, H], U8)
-        nc.vector.memset(w1s_raw[:].bitcast(I32), 0)
+        def load_quadrant(tile, src, q, queue):
+            rows = src[0, 4 * q : 4 * q + 4, :].bitcast(I32)
+            queue.dma_start(tile[32 * q : 32 * (q + 1), :].bitcast(I32), rows.unsqueeze(0).broadcast_to([8, 4, rows.shape[1]]))
 
-        w1w_raw = sb("w1w_raw", [P, 2 * H], U8)
-        nc.gpsimd.dma_start(w1w_raw[:].bitcast(I32), w1_words[0].bitcast(I32))
+        ds_win = load_scale_window("ds_win", d_scales, G, nc.gpsimd)
+        gs_t = sb("gs_t", [P, 4], F32)
+        nc.gpsimd.dma_start(gs_t[:], gs.rearrange("(p t) o -> p (t o)", t=4))
+
         offs_t = load_list("offs_t", offs)
-        xs_win = load_scale_window("xs_win", x_scales, T)
+        xs_win = sb("xs_win", [P, T], U8)
+        w1s_raw = sb("w1s_raw", [P, H], U8)
+        for q in range(4):
+            load_quadrant(xs_win, x_scales, q, nc.sync)
+        for q in range(2):
+            load_quadrant(w1s_raw, w1_scales, q, nc.sync)
+        xw_win = load_words("xw_win", x_words, T)
+        for q in range(2, 4):
+            load_quadrant(w1s_raw, w1_scales, q, nc.sync)
+        w1w_raw = sb("w1w_raw", [P, 2 * H], U8)
+        nc.sync.dma_start(w1w_raw[:].bitcast(I32), w1_words[0].bitcast(I32))
         hz_t = load_list("hz_t", hz)
-        ds_win = load_scale_window("ds_win", d_scales, G)
         k1_t = load_list("k1_t", k1)
         k2_t = load_list("k2_t", k2)
-        xw_win = load_words("xw_win", x_words, T)
         dw_win = load_words("dw_win", d_words, G)
-        for j in range(4):
-            nc.scalar.dma_start(w1s_raw[j:P:32, :].bitcast(I32), w1_scales[0, j:16:4, :].bitcast(I32))
         n1_t = load_list("n1_t", n1)
         n2_t = load_list("n2_t", n2)
-        gs_t = sb("gs_t", [P, 4], F32)
-        nc.sync.dma_start(gs_t[:], gs.rearrange("(p t) o -> p (t o)", t=4))
         n3_t = load_list("n3_t", n3)
 
         def gather(dst, window, lst):
@@ -76,15 +83,11 @@ def tile_picked_cmixhiswapd_none_p_kernel(
             plane = sb(name, [P, cols], U8)
             nc.vector.tensor_copy(plane[:].bitcast(I32), picked[:].bitcast(I32))
             for j in range(1, 4):
-                queue.dma_start(plane[j:P:32, :].bitcast(I32), picked[8 * j : P : 32, :].bitcast(I32))
+                queue.dma_start(plane[j:P:32, :].bitcast(I32), picked[9 * j : P : 32, :].bitcast(I32))
             return plane
 
-        xq_pick = sb("xq_pick", [P, S], U8)
-        gather(xq_pick[:], xs_win, offs_t[:])
-        xq_s = place_scales("xq_s", xq_pick, S, nc.scalar)
-
-        first_pick = sb("first_pick", [P, S + 2 * HALF], U8)
-        gather(first_pick[:, 0:S], xs_win, hz_t[:])
+        xq_s = sb("xq_s", [P, S], U8)
+        gather(xq_s[:], xs_win, offs_t[:])
         xq_w = sb("xq_w", [P, S], U32)
         gather(xq_w[:], xw_win, offs_t[:])
 
@@ -97,9 +100,11 @@ def tile_picked_cmixhiswapd_none_p_kernel(
         nc.vector.tensor_copy(w1s[:].rearrange("p (t m) -> p t m", t=4), w1s_raw[:].rearrange("p (m t) -> p t m", t=4))
 
         lc = HALF // 16
+        first_pick = sb("first_pick", [P, S + 2 * HALF], U8)
+        gather(first_pick[:, 0:S], xs_win, hz_t[:])
         gather(first_pick[:, S : S + HALF], ds_win, k1_t[:, 0:lc])
         gather(first_pick[:, S + HALF :], ds_win, k2_t[:, 0:lc])
-        first_s = place_scales("first_s", first_pick, S + 2 * HALF, nc.scalar)
+        first_s = place_scales("first_s", first_pick, S + 2 * HALF, nc.sync)
 
         z_rows = sb("z_rows", [P, 4, S], BF16)
         for t in range(4):
@@ -114,34 +119,37 @@ def tile_picked_cmixhiswapd_none_p_kernel(
                 stop=True,
             )
             nc.scalar.activation(z_rows[:, t, :], y[:], COPY, scale=gs_t[:, t : t + 1])
-        z_packed = sb("z_packed", [P, S, 4], BF16)
+        z_packed = sb("z_packed", [P, S, 4], BF16, tag="z_then_words")
         nc.scalar.copy(z_packed[:], z_rows[:].rearrange("p t n -> p n t"))
 
         xh_w = sb("xh_w", [P, S], U32)
         gather(xh_w[:], xw_win, hz_t[:])
-        d1_w = [sb(f"d1_w{u}", [P, HALF], U32) for u in range(2)]
-        d2_w = [sb(f"d2_w{u}", [P, HALF], U32) for u in range(2)]
-        gather(d2_w[0][:], dw_win, k2_t[:, 0:lc])
-        gather(d1_w[0][:], dw_win, k1_t[:, 0:lc])
+        first_w = sb("first_w", [P, 2 * HALF], U32, tag="d_picked")
+        gather(first_w[:, HALF:], dw_win, k2_t[:, 0:lc])
+        gather(first_w[:, 0:HALF], dw_win, k1_t[:, 0:lc])
 
         z_w = sb("z_w", [P, S], U32)
         z_s = sb("z_s", [P, S], U8)
         nc.vector.quantize_mx(out=z_w[:].bitcast(FP8X4), scales=z_s[:], in_=z_packed[:].rearrange("p n t -> p (n t)"))
 
-        def second_product(i, d1_s, d2_s):
-            u, c = divmod(i, 2)
+        def second_product(i, d_w, d_s):
+            c = i % 2
+            cols2 = slice(HALF + P * c, HALF + P * (c + 1))
             cols = slice(P * c, P * (c + 1))
             acc = psum.tile([P, S], F32, name=f"h{i}")
             nc.tensor.matmul_mx(
-                out=acc[:], lhsT=d2_w[u][:, cols].bitcast(FP8X4), lhsT_scale=d2_s[:, cols],
+                out=acc[:], lhsT=d_w[:, cols2].bitcast(FP8X4), lhsT_scale=d_s[:, cols2],
                 rhs=xh_w[:].bitcast(FP8X4), rhs_scale=first_s[:, 0:S], start=True, stop=False,
             )
             nc.tensor.matmul_mx(
-                out=acc[:], lhsT=d1_w[u][:, cols].bitcast(FP8X4), lhsT_scale=d1_s[:, cols],
+                out=acc[:], lhsT=d_w[:, cols].bitcast(FP8X4), lhsT_scale=d_s[:, cols],
                 rhs=z_w[:].bitcast(FP8X4), rhs_scale=z_s[:], start=False, stop=True,
             )
             h = sb(f"h_sb{i}", [P, S], F32)
-            nc.vector.tensor_scalar_mul(h[:], acc[:], 0.0625)
+            if i == 0:
+                nc.scalar.activation(h[:], acc[:], COPY, scale=0.0625)
+            else:
+                nc.vector.tensor_scalar_mul(h[:], acc[:], 0.0625)
             return h
 
         def fetch_pairs(i, h):
@@ -153,34 +161,40 @@ def tile_picked_cmixhiswapd_none_p_kernel(
             nc.vector.tensor_tensor(rb[:], pa[:], pb[:], ALU.subtract)
             return pb, rb
 
-        def put_back(i, pb, rb):
-            dt = sb(f"dt{i}", [P, S + SPARE], F32)
-            nc.gpsimd.memset(dt[:, S:], 0.0)
-            nc.scalar.activation(dt[:].indirect(n1_t[:]), pb[:], COPY)
-            nc.scalar.activation(dt[:].indirect(n2_t[:]), rb[:], COPY)
-            return dt
+        def put_back(tiles, pairs):
+            dts = [sb(f"dt{i}", [P, S + SPARE], F32) for i in tiles]
+            for dt in dts:
+                nc.vector.memset(dt[:, S:], 0.0)
+            for dt, (pb, rb) in zip(dts, pairs):
+                nc.scalar.activation(dt[:].indirect(n1_t[:]), pb[:], COPY)
+            for dt, (pb, rb) in zip(dts, pairs):
+                nc.scalar.activation(dt[:].indirect(n2_t[:]), rb[:], COPY)
+            fars = [sb(f"far{i}", [P, S], F32) for i in tiles]
+            for dt, far in zip(dts, fars):
+                nc.scalar.activation(far[:], dt[:].indirect(n3_t[:]), COPY)
+            return dts, fars
 
-        def finish(i, dt):
-            far = sb(f"far{i}", [P, S], F32)
-            nc.scalar.activation(far[:], dt[:].indirect(n3_t[:]), COPY)
-            res = sb(f"res{i}", [P, S], F32)
+        def finish(i, dt, far, tag=None):
+            res = sb(f"res{i}", [P, S], F32, tag=tag)
             nc.vector.scalar_tensor_tensor(res[:], far[:], 0.5, dt[:, 0:S], ALU.mult, ALU.max)
             nc.sync.dma_start(out[P * i : P * (i + 1), :], res[:])
 
-        hs = [second_product(i, first_s[:, S : S + HALF], first_s[:, S + HALF :]) for i in range(2)]
+        hs = [second_product(i, first_w, first_s[:, S:]) for i in range(2)]
         pairs = [fetch_pairs(i, hs[i]) for i in range(2)]
 
-        second_pick = sb("second_pick", [P, 2 * HALF], U8)
+        second_pick = sb("second_pick", [P, 2 * HALF], U8, tag="z_then_words")
         gather(second_pick[:, 0:HALF], ds_win, k1_t[:, lc:])
         gather(second_pick[:, HALF:], ds_win, k2_t[:, lc:])
         second_s = place_scales("second_s", second_pick, 2 * HALF, nc.sync)
-        gather(d2_w[1][:], dw_win, k2_t[:, lc:])
-        gather(d1_w[1][:], dw_win, k1_t[:, lc:])
+        second_w = sb("second_w", [P, 2 * HALF], U32, tag="d_picked")
+        gather(second_w[:, HALF:], dw_win, k2_t[:, lc:])
+        gather(second_w[:, 0:HALF], dw_win, k1_t[:, lc:])
 
-        dts = [put_back(i, *pairs[i]) for i in range(2)]
-        for i in range(2):
-            finish(i, dts[i])
-        hs = [second_product(i, second_s[:, 0:HALF], second_s[:, HALF:]) for i in range(2, 4)]
+        dts, fars = put_back(range(2), pairs)
+        hs = [second_product(i, second_w, second_s) for i in range(2, 4)]
+        finish(0, dts[0], fars[0], tag="d_picked")
+        finish(1, dts[1], fars[1], tag="second_s")
         pairs = [fetch_pairs(i, hs[i - 2]) for i in range(2, 4)]
+        dts, fars = put_back(range(2, 4), pairs)
         for i in range(2, 4):
-            finish(i, put_back(i, *pairs[i - 2]))
+            finish(i, dts[i - 2], fars[i - 2])

from contextlib import ExitStack

import concourse.mybir as mybir

K, T, S, H, G, W = 512, 1024, 256, 512, 2048, 128
FLOPS = 3 * 2 * K * H * S

F32 = mybir.dt.float32
BF16 = mybir.dt.bfloat16
I32 = mybir.dt.int32
U32 = mybir.dt.uint32
U16 = mybir.dt.uint16
U8 = mybir.dt.uint8
FP8X4 = mybir.dt.float8_e4m3fn_x4
FP4X4 = mybir.dt.float4_e2m1fn_x4
COPY = mybir.ActivationFunctionType.Copy
ALU = mybir.AluOpType

P = 128
HALF = 256
SPARE = 8


def tile_picked_cmixhiswapd_none_p_kernel(
    tc, x_words, x_scales, w1_words, w1_scales, gs, d_words, d_scales, offs, k1, k2, hz, n1, n2, n3, out
):
    nc = tc.nc
    with ExitStack() as ctx:
        keep = ctx.enter_context(tc.tile_pool(name="keep", bufs=1))
        psum = ctx.enter_context(tc.psum_pool(name="psum", bufs=1))

        def sb(name, shape, dtype, tag=None):
            return keep.tile(shape, dtype, name=name, tag=tag or name, align_bytes=64)

        def load_list(name, src):
            t = keep.tile(list(src.shape), U16, name=name)
            nc.sync.dma_start(t[:], src)
            return t

        def load_scale_window(name, src, cols, queue):
            t = sb(name, [P, cols], U8)
            rows = src[0].bitcast(I32).unsqueeze(1).broadcast_to([16, 8, cols // 4])
            queue.dma_start(t[:].bitcast(I32), rows)
            return t

        def load_words(name, src, cols, tag=None):
            t = sb(name, [P, cols], U32, tag=tag)
            nc.sync.dma_start(t[:].bitcast(I32), src[0].rearrange("p n t -> p (n t)").bitcast(I32))
            return t

        def load_quadrant(tile, src, q, queue):
            rows = src[0, 4 * q : 4 * q + 4, :].bitcast(I32)
            queue.dma_start(tile[32 * q : 32 * (q + 1), :].bitcast(I32), rows.unsqueeze(0).broadcast_to([8, 4, rows.shape[1]]))

        ds_win = load_scale_window("ds_win", d_scales, G, nc.gpsimd)
        gs_t = sb("gs_t", [P, 4], F32)
        nc.gpsimd.dma_start(gs_t[:], gs.rearrange("(p t) o -> p (t o)", t=4))

        offs_t = load_list("offs_t", offs)
        xs_win = sb("xs_win", [P, T], U8)
        w1s_raw = sb("w1s_raw", [P, H], U8)
        for q in range(4):
            load_quadrant(xs_win, x_scales, q, nc.sync)
        for q in range(2):
            load_quadrant(w1s_raw, w1_scales, q, nc.sync)
        xw_win = load_words("xw_win", x_words, T)
        for q in range(2, 4):
            load_quadrant(w1s_raw, w1_scales, q, nc.sync)
        w1w_raw = sb("w1w_raw", [P, 2 * H], U8)
        nc.sync.dma_start(w1w_raw[:].bitcast(I32), w1_words[0].bitcast(I32))
        hz_t = load_list("hz_t", hz)
        k1_t = load_list("k1_t", k1)
        k2_t = load_list("k2_t", k2)
        dw_win = load_words("dw_win", d_words, G)
        n1_t = load_list("n1_t", n1)
        n2_t = load_list("n2_t", n2)
        n3_t = load_list("n3_t", n3)

        def gather(dst, window, lst):
            nc.vector.tensor_copy(dst, window[:].indirect(lst))

        def place_scales(name, picked, cols, queue):
            plane = sb(name, [P, cols], U8)
            nc.vector.tensor_copy(plane[:].bitcast(I32), picked[:].bitcast(I32))
            for j in range(1, 4):
                queue.dma_start(plane[j:P:32, :].bitcast(I32), picked[9 * j : P : 32, :].bitcast(I32))
            return plane

        xq_s = sb("xq_s", [P, S], U8)
        gather(xq_s[:], xs_win, offs_t[:])
        xq_w = sb("xq_w", [P, S], U32)
        gather(xq_w[:], xw_win, offs_t[:])

        w1w = sb("w1w", [P, 2 * H], U8)
        nc.scalar.copy(
            w1w[:].bitcast(U16).rearrange("p (t m) -> p t m", t=4),
            w1w_raw[:].bitcast(U16).rearrange("p (m t) -> p t m", t=4),
        )
        w1s = sb("w1s", [P, H], U8)
        nc.vector.tensor_copy(w1s[:].rearrange("p (t m) -> p t m", t=4), w1s_raw[:].rearrange("p (m t) -> p t m", t=4))

        lc = HALF // 16
        first_pick = sb("first_pick", [P, S + 2 * HALF], U8)
        gather(first_pick[:, 0:S], xs_win, hz_t[:])
        gather(first_pick[:, S : S + HALF], ds_win, k1_t[:, 0:lc])
        gather(first_pick[:, S + HALF :], ds_win, k2_t[:, 0:lc])
        first_s = place_scales("first_s", first_pick, S + 2 * HALF, nc.sync)

        z_rows = sb("z_rows", [P, 4, S], BF16)
        for t in range(4):
            y = psum.tile([P, S], F32, name=f"y{t}")
            nc.tensor.matmul_mx(
                out=y[:],
                lhsT=w1w[:, 2 * P * t : 2 * P * (t + 1)].bitcast(FP4X4),
                lhsT_scale=w1s[:, P * t : P * (t + 1)],
                rhs=xq_w[:].bitcast(FP8X4),
                rhs_scale=xq_s[:],
                start=True,
                stop=True,
            )
            nc.scalar.activation(z_rows[:, t, :], y[:], COPY, scale=gs_t[:, t : t + 1])
        z_packed = sb("z_packed", [P, S, 4], BF16, tag="z_then_words")
        nc.scalar.copy(z_packed[:], z_rows[:].rearrange("p t n -> p n t"))

        xh_w = sb("xh_w", [P, S], U32)
        gather(xh_w[:], xw_win, hz_t[:])
        first_w = sb("first_w", [P, 2 * HALF], U32, tag="d_picked")
        gather(first_w[:, HALF:], dw_win, k2_t[:, 0:lc])
        gather(first_w[:, 0:HALF], dw_win, k1_t[:, 0:lc])

        z_w = sb("z_w", [P, S], U32)
        z_s = sb("z_s", [P, S], U8)
        nc.vector.quantize_mx(out=z_w[:].bitcast(FP8X4), scales=z_s[:], in_=z_packed[:].rearrange("p n t -> p (n t)"))

        def second_product(i, d_w, d_s):
            c = i % 2
            cols2 = slice(HALF + P * c, HALF + P * (c + 1))
            cols = slice(P * c, P * (c + 1))
            acc = psum.tile([P, S], F32, name=f"h{i}")
            nc.tensor.matmul_mx(
                out=acc[:], lhsT=d_w[:, cols2].bitcast(FP8X4), lhsT_scale=d_s[:, cols2],
                rhs=xh_w[:].bitcast(FP8X4), rhs_scale=first_s[:, 0:S], start=True, stop=False,
            )
            nc.tensor.matmul_mx(
                out=acc[:], lhsT=d_w[:, cols].bitcast(FP8X4), lhsT_scale=d_s[:, cols],
                rhs=z_w[:].bitcast(FP8X4), rhs_scale=z_s[:], start=False, stop=True,
            )
            h = sb(f"h_sb{i}", [P, S], F32)
            if i == 0:
                nc.scalar.activation(h[:], acc[:], COPY, scale=0.0625)
            else:
                nc.vector.tensor_scalar_mul(h[:], acc[:], 0.0625)
            return h

        def fetch_pairs(i, h):
            pb = sb(f"pb{i}", [P, W], F32)
            pa = sb(f"pa{i}", [P, W], F32)
            rb = sb(f"rb{i}", [P, W], F32)
            nc.scalar.activation(pb[:], h[:].indirect(n2_t[:]), COPY)
            nc.scalar.activation(pa[:], h[:].indirect(n1_t[:]), COPY)
            nc.vector.tensor_tensor(rb[:], pa[:], pb[:], ALU.subtract)
            return pb, rb

        def put_back(tiles, pairs):
            dts = [sb(f"dt{i}", [P, S + SPARE], F32) for i in tiles]
            for dt in dts:
                nc.vector.memset(dt[:, S:], 0.0)
            for dt, (pb, rb) in zip(dts, pairs):
                nc.scalar.activation(dt[:].indirect(n1_t[:]), pb[:], COPY)
            for dt, (pb, rb) in zip(dts, pairs):
                nc.scalar.activation(dt[:].indirect(n2_t[:]), rb[:], COPY)
            fars = [sb(f"far{i}", [P, S], F32) for i in tiles]
            for dt, far in zip(dts, fars):
                nc.scalar.activation(far[:], dt[:].indirect(n3_t[:]), COPY)
            return dts, fars

        def finish(i, dt, far, tag=None):
            res = sb(f"res{i}", [P, S], F32, tag=tag)
            nc.vector.scalar_tensor_tensor(res[:], far[:], 0.5, dt[:, 0:S], ALU.mult, ALU.max)
            nc.sync.dma_start(out[P * i : P * (i + 1), :], res[:])

        hs = [second_product(i, first_w, first_s[:, S:]) for i in range(2)]
        pairs = [fetch_pairs(i, hs[i]) for i in range(2)]

        second_pick = sb("second_pick", [P, 2 * HALF], U8, tag="z_then_words")
        gather(second_pick[:, 0:HALF], ds_win, k1_t[:, lc:])
        gather(second_pick[:, HALF:], ds_win, k2_t[:, lc:])
        second_s = place_scales("second_s", second_pick, 2 * HALF, nc.sync)
        second_w = sb("second_w", [P, 2 * HALF], U32, tag="d_picked")
        gather(second_w[:, HALF:], dw_win, k2_t[:, lc:])
        gather(second_w[:, 0:HALF], dw_win, k1_t[:, lc:])

        dts, fars = put_back(range(2), pairs)
        hs = [second_product(i, second_w, second_s) for i in range(2, 4)]
        finish(0, dts[0], fars[0], tag="d_picked")
        finish(1, dts[1], fars[1], tag="second_s")
        pairs = [fetch_pairs(i, hs[i - 2]) for i in range(2, 4)]
        dts, fars = put_back(range(2, 4), pairs)
        for i in range(2, 4):
            finish(i, dts[i - 2], fars[i - 2])
